import numpy as np
import ml_dtypes


def mxq(x, axis, fmt="e4m3"):
    dtype, down = {"e4m3": (ml_dtypes.float8_e4m3fn, 7), "e5m2": (ml_dtypes.float8_e5m2, 14)}[fmt]
    v = np.moveaxis(np.asarray(x, np.float32).astype(ml_dtypes.bfloat16).astype(np.float64), axis, -1)
    blocks = v.reshape(v.shape[:-1] + (-1, 32))
    amax = np.abs(blocks).max(-1, keepdims=True)
    byte = np.maximum(np.where(amax > 0, np.frexp(amax)[1] - 1 + 127, 0) - down, 1)
    scale = np.exp2(byte - 127.0)
    codes = (blocks / scale).astype(np.float32).astype(dtype).astype(np.float64)
    return np.moveaxis((codes * scale).reshape(v.shape), -1, axis)


WIDE = False


def mx_kscale(k):
    if not WIDE:
        return np.ones(k)
    levels = np.array([10, -10, 5, -5, 0])
    if k % 512:
        return np.exp2(np.random.permutation(np.resize(levels, k // 32))).repeat(32)
    a = np.empty((k // 512, 16))
    for p in range(k // 512):
        a[p, :8] = np.random.permutation(np.resize(levels, 8))
        for g in range(8):
            far = levels[np.abs(levels - a[p, g]) >= 10]
            a[p, g + 8] = far[np.random.randint(len(far))]
    return np.exp2(a.ravel()).repeat(32)


def f64(x):
    return np.asarray(x).astype(np.float64)


def striped(idx):
    return np.tile(idx.reshape(-1, 16).T, (8, 1)).astype(np.uint16)


def unstriped(offs):
    return offs[:16].T.reshape(-1).astype(np.int64)


def striped8(idx):
    return np.concatenate([x.reshape(-1, 16).T for x in idx]).astype(np.uint16)


def runs(offs, k):
    lists = np.stack([offs[16 * r : 16 * r + 16].T.reshape(-1) for r in range(8)]).astype(np.int64)
    return lists[np.arange(k) % 512 // 64]


def pack_weight(w):
    k, n = w.shape
    w = f64(np.asarray(w, np.float32).astype(ml_dtypes.bfloat16)).reshape(k // 32, 32, n)
    amax = np.abs(w).max(1)
    byte = np.clip(np.where(amax > 0, np.frexp(amax)[1] - 1 + 127 - 7, 1), 1, 254)
    scaled = (w * np.exp2(127.0 - byte)[:, None, :]).reshape(k, n).astype(np.float32)
    words = np.ascontiguousarray(scaled.reshape(k // 512, 128, 4, n).transpose(0, 1, 3, 2)).astype(ml_dtypes.float8_e4m3fn).view(np.uint8)
    return words, np.ascontiguousarray(byte.astype(np.uint8).reshape(k // 512, 16, n))


def unpack_weight(words, scales):
    g, p, n, _ = words.shape
    vals = np.ascontiguousarray(words).view(ml_dtypes.float8_e4m3fn).astype(np.float64) * np.repeat(np.exp2(scales.astype(np.float64) - 127.0), 8, axis=1)[..., None]
    return vals.transpose(0, 1, 3, 2).reshape(g * 512, n)


def sigmoid(v):
    return 1.0 / (1.0 + np.exp(-np.maximum(v, -700.0)))


K, T, S, H, W, G = 512, 1024, 256, 512, 128, 2048


def setup_inputs():
    n = np.random.standard_normal
    s = mx_kscale(K)[:, None]
    packed_xT = pack_weight(n((K, T)) * s)
    packed_w1 = pack_weight(n((K, H)) / np.sqrt(2 * K) / s)
    packed_w2 = pack_weight(n((K, H)) / np.sqrt(2 * K) / s)
    packed_dT = pack_weight(n((K, G)) / s)
    perm = np.random.permutation(S)
    perm2 = np.random.permutation(S)
    perm3 = np.random.permutation(S)
    return {
        "x_words": packed_xT[0],
        "x_scales": packed_xT[1],
        "w1_words": packed_w1[0],
        "w1_scales": packed_w1[1],
        "w2_words": packed_w2[0],
        "w2_scales": packed_w2[1],
        "gs": (np.random.uniform(0.5, 1.5, (K, 1)) * s).astype(np.float32),
        "d_words": packed_dT[0],
        "d_scales": packed_dT[1],
        "sl": np.random.uniform(1.0, 2.0, (H, 1)).astype(np.float32),
        "th": (0.5 * n((H, 1))).astype(np.float32),
        "offs": striped8(np.random.randint(0, T, (8, S))),
        "hz": striped8(np.random.randint(0, T, (8, S))),
        "n1": striped(perm[:W]),
        "n2": striped(perm[W:]),
        "k1": striped8(np.random.randint(0, G, (8, H))),
        "k2": striped8(np.random.randint(0, G, (8, H))),
        "two": striped(np.random.permutation(T)[:S]),
        "k3": striped8(np.random.randint(0, G, (8, H))),
        "hy": striped8(np.random.randint(0, T, (8, S))),
        "n3": striped(np.random.permutation(S)),
        "n4": striped(perm2[:W]),
        "n5": striped(perm2[W:]),
        "n6": striped(perm3[:W]),
        "n7": striped(perm3[W:]),
    }


def reference(x_words, x_scales, w1_words, w1_scales, w2_words, w2_scales, gs, d_words, d_scales, sl, th, offs, hz, n1, n2, k1, k2, two, k3, hy, n3, n4, n5, n6, n7):
    d_k1 = unpack_weight(d_words, d_scales)[np.arange(K)[:, None], runs(k1, K)]
    xq = unpack_weight(x_words, x_scales)[np.arange(K)[:, None], runs(offs, K)]
    x_hz = unpack_weight(x_words, x_scales)[np.arange(K)[:, None], runs(hz, K)]
    y = unpack_weight(w1_words, w1_scales).T @ xq + unpack_weight(w2_words, w2_scales).T @ x_hz
    pb = y[:, unstriped(n2)]
    pa = y[:, unstriped(n1)]
    rb = pb - (0.5 * pa)
    ra = np.sqrt((pa) ** 2 + (pb) ** 2 + 0.25)
    ua = np.zeros((H, S))
    ua[:, unstriped(n1)] = ra
    ub = ua.copy()
    ub[:, unstriped(n2)] = rb
    z = f64(gs) * ub
    d_k2 = unpack_weight(d_words, d_scales)[np.arange(K)[:, None], runs(k2, K)]
    x_two = unpack_weight(x_words, x_scales)[:, unstriped(two)]
    d_k3 = unpack_weight(d_words, d_scales)[np.arange(K)[:, None], runs(k3, K)]
    x_hy = unpack_weight(x_words, x_scales)[np.arange(K)[:, None], runs(hy, K)]
    h2 = 0.0625 * ((d_k1.T @ mxq(z, 0, "e4m3") + d_k2.T @ x_two + d_k3.T @ x_hy))
    sg = sigmoid(f64(sl) * (h2[:, unstriped(n3)] - f64(th)))
    st = h2 * sg
    pa2 = st[:, unstriped(n4)]
    pb2 = st[:, unstriped(n5)]
    rb2 = pa2 - pb2
    ra2 = np.maximum(pa2, pb2)
    ua2 = np.zeros((H, S))
    ua2[:, unstriped(n6)] = ra2
    out = ua2.copy()
    out[:, unstriped(n7)] = rb2
    return out

@@ -1,0 +1,276 @@
+from contextlib import ExitStack
+
+import concourse.mybir as mybir
+
+K, T, S, H, W, G = 512, 1024, 256, 512, 128, 2048
+FLOPS = 5 * 2 * K * H * S
+
+F32 = mybir.dt.float32
+BF16 = mybir.dt.bfloat16
+I32 = mybir.dt.int32
+U32 = mybir.dt.uint32
+U16 = mybir.dt.uint16
+U8 = mybir.dt.uint8
+FP8X4 = mybir.dt.float8_e4m3fn_x4
+ALU = mybir.AluOpType
+ACT = mybir.ActivationFunctionType
+
+P = 128
+TILES = 4
+HALF = 256
+
+
+def tile_picked_dhhzmthpolarecpx_none_p_kernel(
+    tc, x_words, x_scales, w1_words, w1_scales, w2_words, w2_scales, gs, d_words, d_scales, sl, th,
+    offs, hz, n1, n2, k1, k2, two, k3, hy, n3, n4, n5, n6, n7, out,
+):
+    nc = tc.nc
+    with ExitStack() as ctx:
+        lists = ctx.enter_context(tc.tile_pool(name="lists", bufs=1))
+        sb = ctx.enter_context(tc.tile_pool(name="sb", bufs=1))
+        psum = ctx.enter_context(tc.psum_pool(name="psum", bufs=1))
+
+        def tile(name, cols, dtype, tag=None):
+            return sb.tile([P, cols], dtype, name=name, tag=tag or name, align_bytes=64)
+
+        def load_list(name, src):
+            t = lists.tile(list(src.shape), U16, name="list_" + name, tag="list_" + name)
+            nc.sync.dma_start(t[:], src)
+            return t
+
+        def load_words(name, src, tag=None):
+            t = tile(name, src.shape[2], U32, tag)
+            nc.sync.dma_start(t[:].bitcast(I32), src[0].rearrange("p n t -> p (n t)").bitcast(I32))
+            return t
+
+        def load_scale_table(name, src, tag=None):
+            cols = src.shape[2]
+            t = tile(name, cols, U8, tag)
+            rows = src[0].bitcast(I32)
+            nc.sync.dma_start(t[:].bitcast(I32), rows.unsqueeze(1).to_broadcast([16, 8, cols // 4]))
+            return t
+
+        def zeroed_plane(name, cols):
+            t = tile(name, cols, U8)
+            nc.vector.memset(t[:].bitcast(I32), 0)
+            return t
+
+        def move_rows(plane, picked, queues):
+            for q in range(4):
+                queues[q % len(queues)].dma_start(
+                    plane[32 * q : 32 * q + 4, :].bitcast(I32), picked[32 * q : 32 * q + 32 : 8, :].bitcast(I32)
+                )
+
+        def gather(dst, table, offsets):
+            nc.vector.tensor_copy(dst, table[:].indirect(offsets))
+
+        xs = load_scale_table("xs", x_scales)
+        l_offs = load_list("offs", offs)
+        l_hz = load_list("hz", hz)
+        ws_raw = [load_scale_table(name, src) for name, src in (("w1s_raw", w1_scales), ("w2s_raw", w2_scales))]
+        l_n1 = load_list("n1", n1)
+        l_n2 = load_list("n2", n2)
+        xw = load_words("xw", x_words)
+        w1_raw = load_words("w1_raw", w1_words)
+        w2_raw = load_words("w2_raw", w2_words)
+        l_two = load_list("two", two)
+        l_hy = load_list("hy", hy)
+        l_k = [load_list(name, src) for name, src in (("k1", k1), ("k2", k2), ("k3", k3))]
+        l_n3 = load_list("n3", n3)
+        l_n4 = load_list("n4", n4)
+        l_n5 = load_list("n5", n5)
+        l_n6 = load_list("n6", n6)
+        l_n7 = load_list("n7", n7)
+        plane_y = zeroed_plane("plane_y", 2 * S + 2 * H)
+        plane_x = zeroed_plane("plane_x", 2 * S)
+        plane_a = zeroed_plane("plane_a", 5 * HALF)
+        plane_b = zeroed_plane("plane_b", HALF)
+
+        picked_offs = tile("picked_offs", S, U8, "hold_ds")
+        picked_hz = tile("picked_hz", S, U8, "hold_dw")
+        gather(picked_offs[:], xs, l_offs[:])
+        gather(picked_hz[:], xs, l_hz[:])
+        stage = tile("stage", 2 * S + 2 * H, U8)
+        for i, raw in enumerate(ws_raw):
+            dealt = stage[:, 2 * S + i * H : 2 * S + (i + 1) * H]
+            nc.vector.tensor_copy(dealt.rearrange("p (t m) -> p m t", t=TILES), raw[:].rearrange("p (m t) -> p m t", t=TILES))
+        nc.vector.tensor_copy(stage[:, 0:S], picked_offs[:])
+        nc.vector.tensor_copy(stage[:, S : 2 * S], picked_hz[:])
+        move_rows(plane_y, stage, [nc.sync])
+        ds = load_scale_table("ds", d_scales, "hold_ds")
+        dw = load_words("dw", d_words, "hold_dw")
+
+        x_offs = tile("x_offs", S, U32)
+        x_hz = tile("x_hz", S, U32)
+        gather(x_offs[:], xw, l_offs[:])
+        gather(x_hz[:], xw, l_hz[:])
+        w1 = tile("w1", H, U32)
+        w2 = tile("w2", H, U32)
+        for dealt, raw in ((w1, w1_raw), (w2, w2_raw)):
+            nc.scalar.copy(dealt[:].rearrange("p (t m) -> p m t", t=TILES), raw[:].rearrange("p (m t) -> p m t", t=TILES))
+
+        y_ps = []
+        for t in range(TILES):
+            acc = psum.tile([P, S], F32, name=f"y_ps{t}", tag=f"y_ps{t}")
+            cols = slice(t * P, (t + 1) * P)
+            nc.tensor.matmul_mx(acc[:], lhsT=w1[:, cols].bitcast(FP8X4), lhsT_scale=plane_y[:, 2 * S + t * P : 2 * S + (t + 1) * P],
+                                rhs=x_offs[:].bitcast(FP8X4), rhs_scale=plane_y[:, 0:S], start=True, stop=False)
+            nc.tensor.matmul_mx(acc[:], lhsT=w2[:, cols].bitcast(FP8X4), lhsT_scale=plane_y[:, 2 * S + H + t * P : 2 * S + H + (t + 1) * P],
+                                rhs=x_hz[:].bitcast(FP8X4), rhs_scale=plane_y[:, S : 2 * S], start=False, stop=True)
+            y_ps.append(acc)
+
+        gs_t = tile("gs_t", TILES, F32, "x_offs")
+        sl_t = tile("sl_t", TILES, F32, "x_hz")
+        th_t = tile("th_t", TILES, F32, "w1")
+        nc.sync.dma_start(gs_t[:], gs.rearrange("(p t) o -> p (t o)", t=TILES))
+        with nc.allow_non_contiguous_dma(reason="one value a row, rows 128 t + p"):
+            nc.sync.dma_start(sl_t[:], sl.rearrange("(t p) o -> p (t o)", t=TILES))
+            nc.sync.dma_start(th_t[:], th.rearrange("(t p) o -> p (t o)", t=TILES))
+
+        x_two = tile("x_two", S, U32)
+        x_hy = tile("x_hy", S, U32)
+        picked_x = tile("picked_x", 2 * S, U8)
+        gather(picked_x[:, 0:S], xs, l_two[:])
+        gather(picked_x[:, S : 2 * S], xs, l_hy[:])
+        move_rows(plane_x, picked_x, [nc.sync])
+        gather(x_two[:], xw, l_two[:])
+        gather(x_hy[:], xw, l_hy[:])
+
+        z = tile("z", TILES * S, BF16)
+        z_view = z[:].rearrange("p (j t) -> p j t", t=TILES)
+        pairs, roots, rests, ubs = {}, {}, {}, {}
+
+        def fetch_y(t):
+            y = tile(f"y{t}", S, F32)
+            if t == 0:
+                nc.scalar.copy(y[:], y_ps[t][:])
+            else:
+                nc.vector.tensor_copy(y[:], y_ps[t][:])
+            pair = tile(f"pair{t}", 2 * W, F32)
+            nc.scalar.activation(pair[:, 0:W], y[:].indirect(l_n1[:]), ACT.Copy)
+            nc.scalar.activation(pair[:, W : 2 * W], y[:].indirect(l_n2[:]), ACT.Copy)
+            pairs[t] = pair
+
+        def polar(t):
+            pair = pairs[t]
+            sq = tile(f"sq{t}", 2 * W, F32)
+            nc.vector.tensor_tensor(sq[:], pair[:], pair[:], ALU.mult)
+            rest = tile(f"rest{t}", W, F32)
+            nc.vector.scalar_tensor_tensor(rest[:], pair[:, 0:W], -0.5, pair[:, W : 2 * W], ALU.mult, ALU.add)
+            ssum = tile(f"ssum{t}", W, F32)
+            nc.vector.scalar_tensor_tensor(ssum[:], sq[:, 0:W], 0.25, sq[:, W : 2 * W], ALU.add, ALU.add)
+            roots[t], rests[t] = ssum, rest
+
+        def place_u(t):
+            root = tile(f"root{t}", W, F32)
+            nc.scalar.activation(root[:], roots[t][:], ACT.Sqrt)
+            ub = tile(f"ub{t}", S, F32)
+            nc.scalar.activation(ub[:].indirect(l_n2[:]), rests[t][:], ACT.Copy)
+            nc.scalar.activation(ub[:].indirect(l_n1[:]), root[:], ACT.Copy)
+            ubs[t] = ub
+
+        def weigh(t):
+            nc.vector.tensor_scalar(z_view[:, :, t], ubs[t][:], gs_t[:, t : t + 1], None, ALU.mult)
+
+        def pick_d(name, i, half, tag):
+            dst = tile(name, HALF, U32, tag)
+            gather(dst[:], dw, l_k[i][:, 16 * half : 16 * half + 16])
+            return dst
+
+        fetch_y(0)
+        fetch_y(1)
+        polar(0)
+        place_u(0)
+        polar(1)
+        fetch_y(2)
+        place_u(1)
+        fetch_y(3)
+        polar(2)
+        place_u(2)
+        polar(3)
+        place_u(3)
+
+        picked_a = tile("picked_a", 5 * HALF, U8, "sq1")
+        gather(picked_a[:, 0:H], ds, l_k[0][:])
+        gather(picked_a[:, H : 2 * H], ds, l_k[1][:])
+        gather(picked_a[:, 2 * H : 2 * H + HALF], ds, l_k[2][:, 0:16])
+        move_rows(plane_a, picked_a, [nc.sync])
+        d_a = {i: pick_d(f"d_a{i}", i, 0, tag) for i, tag in ((1, "sq3"), (2, "pair3"), (0, "y3"))}
+
+        bias = tile("bias", TILES, F32)
+        nc.vector.scalar_tensor_tensor(bias[:], sl_t[:], -1.0, th_t[:], ALU.mult, ALU.mult)
+        for t in range(TILES):
+            weigh(t)
+        z_codes = tile("z_codes", S, U32)
+        z_plane = tile("z_plane", S, U8)
+        nc.vector.quantize_mx(out=z_codes[:].bitcast(FP8X4), scales=z_plane[:], in_=z[:])
+
+        picked_b = tile("picked_b", HALF, U8, "z")
+        gather(picked_b[:], ds, l_k[2][:, 16:32])
+        move_rows(plane_b, picked_b, [nc.sync])
+
+        h2s, sts, pairs2, results = {}, {}, {}, {}
+
+        def product(t, d_codes):
+            acc = psum.tile([P, S], F32, name=f"h_ps{t}", tag=f"h_ps{t}")
+            moving = (
+                (1, x_two, plane_x[:, 0:S]),
+                (2, x_hy, plane_x[:, S : 2 * S]),
+                (0, z_codes, z_plane[:]),
+            )
+            for n, (i, codes, plane) in enumerate(moving):
+                c0 = (t % 2) * P
+                if i == 2 and t >= 2:
+                    d_plane = plane_b[:, (t - 2) * P : (t - 1) * P]
+                else:
+                    d_plane = plane_a[:, i * H + t * P : i * H + (t + 1) * P]
+                nc.tensor.matmul_mx(acc[:], lhsT=d_codes[i][:, c0 : c0 + P].bitcast(FP8X4), lhsT_scale=d_plane,
+                                    rhs=codes[:].bitcast(FP8X4), rhs_scale=plane, start=(n == 0), stop=(n == 2))
+            h2 = tile(f"h2_{t}", S, F32)
+            nc.vector.tensor_scalar(h2[:], acc[:], 0.0625, None, ALU.mult)
+            h2s[t] = h2
+
+        def gate(t):
+            sg = tile(f"sg{t}", S, F32)
+            for u in range(2):
+                nc.scalar.activation(sg[:, u * W : (u + 1) * W], h2s[t][:].indirect(l_n3[:, 8 * u : 8 * u + 8]), ACT.Sigmoid,
+                                     bias=bias[:, t : t + 1], scale=sl_t[:, t : t + 1])
+            st = tile(f"st{t}", S, F32)
+            nc.vector.tensor_tensor(st[:], h2s[t][:], sg[:], ALU.mult)
+            sts[t] = st
+
+        def fetch_st(t):
+            pair = tile(f"pair2_{t}", 2 * W, F32)
+            nc.scalar.activation(pair[:, 0:W], sts[t][:].indirect(l_n4[:]), ACT.Copy)
+            nc.scalar.activation(pair[:, W : 2 * W], sts[t][:].indirect(l_n5[:]), ACT.Copy)
+            larger = tile(f"larger{t}", W, F32)
+            diff = tile(f"diff{t}", W, F32)
+            nc.vector.tensor_tensor(larger[:], pair[:, 0:W], pair[:, W : 2 * W], ALU.max)
+            nc.vector.tensor_tensor(diff[:], pair[:, 0:W], pair[:, W : 2 * W], ALU.subtract)
+            pairs2[t] = (larger, diff)
+
+        def place_out(t):
+            res = tile(f"res{t}", S, F32)
+            nc.scalar.activation(res[:].indirect(l_n6[:]), pairs2[t][0][:], ACT.Copy)
+            nc.scalar.activation(res[:].indirect(l_n7[:]), pairs2[t][1][:], ACT.Copy)
+            nc.sync.dma_start(out[t * P : (t + 1) * P, :], res[:])
+
+        product(0, d_a)
+        product(1, d_a)
+        gate(0)
+        d_b = {1: pick_d("d_b1", 1, 1, "sg0")}
+        gate(1)
+        fetch_st(0)
+        d_b[2] = pick_d("d_b2", 2, 1, "pair2_0")
+        d_b[0] = pick_d("d_b0", 0, 1, "st0")
+        fetch_st(1)
+        place_out(0)
+        place_out(1)
+        product(2, d_b)
+        product(3, d_b)
+        gate(2)
+        gate(3)
+        fetch_st(2)
+        fetch_st(3)
+        place_out(2)
+        place_out(3)

@@ -64,6 +64,11 @@ def tile_picked_dhhzmthpolarecpx_none_p_kernel(
         def gather(dst, table, offsets):
             nc.vector.tensor_copy(dst, table[:].indirect(offsets))
 
+        warm_in = tile("warm_in", 1, F32)
+        warm_out = tile("warm_out", 1, F32)
+        nc.vector.memset(warm_in[:], 1.0)
+        nc.scalar.activation(warm_out[:], warm_in[:], ACT.Sqrt)
+
         xs = load_scale_table("xs", x_scales)
         l_offs = load_list("offs", offs)
         l_hz = load_list("hz", hz)

@@ -80,12 +80,6 @@ def tile_picked_dhhzmthpolarecpx_none_p_kernel(
         w2_raw = load_words("w2_raw", w2_words)
         l_two = load_list("two", two)
         l_hy = load_list("hy", hy)
-        l_k = [load_list(name, src) for name, src in (("k1", k1), ("k2", k2), ("k3", k3))]
-        l_n3 = load_list("n3", n3)
-        l_n4 = load_list("n4", n4)
-        l_n5 = load_list("n5", n5)
-        l_n6 = load_list("n6", n6)
-        l_n7 = load_list("n7", n7)
         plane_y = zeroed_plane("plane_y", 2 * S + 2 * H)
         plane_x = zeroed_plane("plane_x", 2 * S)
         plane_a = zeroed_plane("plane_a", 5 * HALF)
@@ -102,6 +96,7 @@ def tile_picked_dhhzmthpolarecpx_none_p_kernel(
         nc.vector.tensor_copy(stage[:, 0:S], picked_offs[:])
         nc.vector.tensor_copy(stage[:, S : 2 * S], picked_hz[:])
         move_rows(plane_y, stage, [nc.sync])
+        l_k = [load_list(name, src) for name, src in (("k1", k1), ("k2", k2), ("k3", k3))]
         ds = load_scale_table("ds", d_scales, "hold_ds")
         dw = load_words("dw", d_words, "hold_dw")
 
@@ -124,6 +119,11 @@ def tile_picked_dhhzmthpolarecpx_none_p_kernel(
                                 rhs=x_hz[:].bitcast(FP8X4), rhs_scale=plane_y[:, S : 2 * S], start=False, stop=True)
             y_ps.append(acc)
 
+        l_n3 = load_list("n3", n3)
+        l_n4 = load_list("n4", n4)
+        l_n5 = load_list("n5", n5)
+        l_n6 = load_list("n6", n6)
+        l_n7 = load_list("n7", n7)
         gs_t = tile("gs_t", TILES, F32, "x_offs")
         sl_t = tile("sl_t", TILES, F32, "x_hz")
         th_t = tile("th_t", TILES, F32, "w1")
@@ -143,7 +143,7 @@ def tile_picked_dhhzmthpolarecpx_none_p_kernel(
 
         z = tile("z", TILES * S, BF16)
         z_view = z[:].rearrange("p (j t) -> p j t", t=TILES)
-        pairs, roots, rests, ubs = {}, {}, {}, {}
+        pairs, roots, rests, ubs, wide = {}, {}, {}, {}, {}
 
         def fetch_y(t):
             y = tile(f"y{t}", S, F32)
@@ -160,55 +160,53 @@ def tile_picked_dhhzmthpolarecpx_none_p_kernel(
             pair = pairs[t]
             sq = tile(f"sq{t}", 2 * W, F32)
             nc.vector.tensor_tensor(sq[:], pair[:], pair[:], ALU.mult)
-            rest = tile(f"rest{t}", W, F32)
-            nc.vector.scalar_tensor_tensor(rest[:], pair[:, 0:W], -0.5, pair[:, W : 2 * W], ALU.mult, ALU.add)
+            wide[t] = tile(f"wide{t}", 2 * S, F32)
+            rest = wide[t][:, S : S + W]
+            nc.vector.scalar_tensor_tensor(rest, pair[:, 0:W], -0.5, pair[:, W : 2 * W], ALU.mult, ALU.add)
             ssum = tile(f"ssum{t}", W, F32)
             nc.vector.scalar_tensor_tensor(ssum[:], sq[:, 0:W], 0.25, sq[:, W : 2 * W], ALU.add, ALU.add)
             roots[t], rests[t] = ssum, rest
 
         def place_u(t):
-            root = tile(f"root{t}", W, F32)
-            nc.scalar.activation(root[:], roots[t][:], ACT.Sqrt)
+            root = wide[t][:, S + W : 2 * S]
+            nc.scalar.activation(root, roots[t][:], ACT.Sqrt)
             ub = tile(f"ub{t}", S, F32)
-            nc.scalar.activation(ub[:].indirect(l_n2[:]), rests[t][:], ACT.Copy)
-            nc.scalar.activation(ub[:].indirect(l_n1[:]), root[:], ACT.Copy)
+            nc.scalar.activation(ub[:].indirect(l_n2[:]), rests[t], ACT.Copy)
+            nc.scalar.activation(ub[:].indirect(l_n1[:]), root, ACT.Copy)
             ubs[t] = ub
 
-        def weigh(t):
-            nc.vector.tensor_scalar(z_view[:, :, t], ubs[t][:], gs_t[:, t : t + 1], None, ALU.mult)
+        def weigh(t, cols):
+            nc.vector.tensor_scalar(z_view[:, cols, t], ubs[t][:, cols], gs_t[:, t : t + 1], None, ALU.mult)
 
         def pick_d(name, i, half, tag):
             dst = tile(name, HALF, U32, tag)
             gather(dst[:], dw, l_k[i][:, 16 * half : 16 * half + 16])
             return dst
 
-        fetch_y(0)
-        fetch_y(1)
-        polar(0)
-        place_u(0)
-        polar(1)
-        fetch_y(2)
-        place_u(1)
-        fetch_y(3)
-        polar(2)
-        place_u(2)
-        polar(3)
-        place_u(3)
+        picked_k1 = tile("picked_k1", H, U8)
+        gather(picked_k1[:], ds, l_k[0][:])
+        move_rows(plane_a[:, 0:H], picked_k1, [nc.sync])
+        for step in (fetch_y, polar, place_u):
+            for t in range(TILES):
+                step(t)
 
-        picked_a = tile("picked_a", 5 * HALF, U8, "sq1")
-        gather(picked_a[:, 0:H], ds, l_k[0][:])
-        gather(picked_a[:, H : 2 * H], ds, l_k[1][:])
-        gather(picked_a[:, 2 * H : 2 * H + HALF], ds, l_k[2][:, 0:16])
-        move_rows(plane_a, picked_a, [nc.sync])
-        d_a = {i: pick_d(f"d_a{i}", i, 0, tag) for i, tag in ((1, "sq3"), (2, "pair3"), (0, "y3"))}
+        picked_a = tile("picked_a", 3 * HALF, U8, "sq1")
+        gather(picked_a[:, 0:H], ds, l_k[1][:])
+        gather(picked_a[:, H : H + HALF], ds, l_k[2][:, 0:16])
+        move_rows(plane_a[:, H : 5 * HALF], picked_a, [nc.sync])
+        d_a = {i: pick_d(f"d_a{i}", i, 0, tag) for i, tag in ((1, "sq2"), (2, "pair2"), (0, "pair3"))}
 
         bias = tile("bias", TILES, F32)
         nc.vector.scalar_tensor_tensor(bias[:], sl_t[:], -1.0, th_t[:], ALU.mult, ALU.mult)
-        for t in range(TILES):
-            weigh(t)
+        for t in range(TILES - 1):
+            weigh(t, slice(0, S))
+        weigh(TILES - 1, slice(0, W))
+        weigh(TILES - 1, slice(W, S))
         z_codes = tile("z_codes", S, U32)
         z_plane = tile("z_plane", S, U8)
-        nc.vector.quantize_mx(out=z_codes[:].bitcast(FP8X4), scales=z_plane[:], in_=z[:])
+        for u in range(2):
+            cols = slice(u * W, (u + 1) * W)
+            nc.vector.quantize_mx(out=z_codes[:, cols].bitcast(FP8X4), scales=z_plane[:, cols], in_=z[:, TILES * u * W : TILES * (u + 1) * W])
 
         picked_b = tile("picked_b", HALF, U8, "z")
         gather(picked_b[:], ds, l_k[2][:, 16:32])
@@ -219,29 +217,28 @@ def tile_picked_dhhzmthpolarecpx_none_p_kernel(
         def product(t, d_codes):
             acc = psum.tile([P, S], F32, name=f"h_ps{t}", tag=f"h_ps{t}")
             moving = (
-                (1, x_two, plane_x[:, 0:S]),
-                (2, x_hy, plane_x[:, S : 2 * S]),
-                (0, z_codes, z_plane[:]),
+                (1, x_two[:], plane_x[:, 0:S], slice(0, S)),
+                (2, x_hy[:], plane_x[:, S : 2 * S], slice(0, S)),
+                (0, z_codes[:, 0:W], z_plane[:, 0:W], slice(0, W)),
+                (0, z_codes[:, W:S], z_plane[:, W:S], slice(W, S)),
             )
-            for n, (i, codes, plane) in enumerate(moving):
+            for n, (i, codes, plane, cols) in enumerate(moving):
                 c0 = (t % 2) * P
                 if i == 2 and t >= 2:
                     d_plane = plane_b[:, (t - 2) * P : (t - 1) * P]
                 else:
                     d_plane = plane_a[:, i * H + t * P : i * H + (t + 1) * P]
-                nc.tensor.matmul_mx(acc[:], lhsT=d_codes[i][:, c0 : c0 + P].bitcast(FP8X4), lhsT_scale=d_plane,
-                                    rhs=codes[:].bitcast(FP8X4), rhs_scale=plane, start=(n == 0), stop=(n == 2))
-            h2 = tile(f"h2_{t}", S, F32)
-            nc.vector.tensor_scalar(h2[:], acc[:], 0.0625, None, ALU.mult)
+                nc.tensor.matmul_mx(acc[:, cols], lhsT=d_codes[i][:, c0 : c0 + P].bitcast(FP8X4), lhsT_scale=d_plane,
+                                    rhs=codes.bitcast(FP8X4), rhs_scale=plane, start=(n == 0), stop=(n == 3))
+            h2 = wide[t][:, 0:S]
+            nc.vector.tensor_scalar(h2, acc[:], 0.0625, None, ALU.mult)
             h2s[t] = h2
 
         def gate(t):
             sg = tile(f"sg{t}", S, F32)
-            for u in range(2):
-                nc.scalar.activation(sg[:, u * W : (u + 1) * W], h2s[t][:].indirect(l_n3[:, 8 * u : 8 * u + 8]), ACT.Sigmoid,
-                                     bias=bias[:, t : t + 1], scale=sl_t[:, t : t + 1])
+            nc.scalar.activation(sg[:], wide[t][:].indirect(l_n3[:]), ACT.Sigmoid, bias=bias[:, t : t + 1], scale=sl_t[:, t : t + 1])
             st = tile(f"st{t}", S, F32)
-            nc.vector.tensor_tensor(st[:], h2s[t][:], sg[:], ALU.mult)
+            nc.vector.tensor_tensor(st[:], h2s[t], sg[:], ALU.mult)
             sts[t] = st
 
         def fetch_st(t):
@@ -262,13 +259,13 @@ def tile_picked_dhhzmthpolarecpx_none_p_kernel(
 
         product(0, d_a)
         product(1, d_a)
+        d_b = {1: pick_d("d_b1", 1, 1, "pair3")}
         gate(0)
-        d_b = {1: pick_d("d_b1", 1, 1, "sg0")}
         gate(1)
         fetch_st(0)
         d_b[2] = pick_d("d_b2", 2, 1, "pair2_0")
-        d_b[0] = pick_d("d_b0", 0, 1, "st0")
         fetch_st(1)
+        d_b[0] = pick_d("d_b0", 0, 1, "pair2_1")
         place_out(0)
         place_out(1)
         product(2, d_b)

@@ -2,7 +2,7 @@ from contextlib import ExitStack
 
 import concourse.mybir as mybir
 
-K, T, S, H, W, G = 512, 1024, 256, 512, 128, 2048
+K, S, H, W = 512, 256, 512, 128
 FLOPS = 5 * 2 * K * H * S
 
 F32 = mybir.dt.float32
@@ -17,7 +17,12 @@ ACT = mybir.ActivationFunctionType
 
 P = 128
 TILES = 4
-HALF = 256
+QUADRANTS = 4
+BLOCK_PARTITIONS = 8
+SCALE_ROWS = 16
+HALF = H // 2
+HALF_COLS = HALF // 16
+K1, K2, K3 = 0, 1, 2
 
 
 def tile_picked_dhhzmthpolarecpx_none_p_kernel(
@@ -30,39 +35,45 @@ def tile_picked_dhhzmthpolarecpx_none_p_kernel(
         sb = ctx.enter_context(tc.tile_pool(name="sb", bufs=1))
         psum = ctx.enter_context(tc.psum_pool(name="psum", bufs=1))
 
-        def tile(name, cols, dtype, tag=None):
-            return sb.tile([P, cols], dtype, name=name, tag=tag or name, align_bytes=64)
+        def tile(name, cols, dtype, after=None):
+            return sb.tile([P, cols], dtype, name=name, tag=after or name, align_bytes=64)
 
         def load_list(name, src):
-            t = lists.tile(list(src.shape), U16, name="list_" + name, tag="list_" + name)
-            nc.sync.dma_start(t[:], src)
-            return t
+            offsets = lists.tile(list(src.shape), U16, name="list_" + name, tag="list_" + name)
+            nc.sync.dma_start(offsets[:], src)
+            return offsets
 
-        def load_words(name, src, tag=None):
-            t = tile(name, src.shape[2], U32, tag)
-            nc.sync.dma_start(t[:].bitcast(I32), src[0].rearrange("p n t -> p (n t)").bitcast(I32))
-            return t
+        def load_words(name, src, after=None):
+            words = tile(name, src.shape[2], U32, after)
+            nc.sync.dma_start(words[:].bitcast(I32), src[0].rearrange("p n t -> p (n t)").bitcast(I32))
+            return words
 
-        def load_scale_table(name, src, tag=None):
-            cols = src.shape[2]
-            t = tile(name, cols, U8, tag)
+        def load_scale_rows(dst, src):
             rows = src[0].bitcast(I32)
-            nc.sync.dma_start(t[:].bitcast(I32), rows.unsqueeze(1).to_broadcast([16, 8, cols // 4]))
-            return t
+            nc.sync.dma_start(dst.bitcast(I32), rows.unsqueeze(1).to_broadcast([SCALE_ROWS, BLOCK_PARTITIONS, src.shape[2] // 4]))
+
+        def load_scale_table(name, src, after=None):
+            table = tile(name, src.shape[2], U8, after)
+            load_scale_rows(table[:], src)
+            return table
 
         def zeroed_plane(name, cols):
-            t = tile(name, cols, U8)
-            nc.vector.memset(t[:].bitcast(I32), 0)
-            return t
+            plane = tile(name, cols, U8)
+            nc.vector.memset(plane[:].bitcast(I32), 0)
+            return plane
 
-        def move_rows(plane, picked, queues):
-            for q in range(4):
-                queues[q % len(queues)].dma_start(
-                    plane[32 * q : 32 * q + 4, :].bitcast(I32), picked[32 * q : 32 * q + 32 : 8, :].bitcast(I32)
+        def move_rows(plane, table_layout):
+            for q in range(QUADRANTS):
+                nc.sync.dma_start(
+                    plane[32 * q : 32 * q + 4, :].bitcast(I32),
+                    table_layout[32 * q : 32 * q + 32 : BLOCK_PARTITIONS, :].bitcast(I32),
                 )
 
         def gather(dst, table, offsets):
             nc.vector.tensor_copy(dst, table[:].indirect(offsets))
+
+        def list_half(offsets, half):
+            return offsets[:, half * HALF_COLS : (half + 1) * HALF_COLS]
 
         warm_in = tile("warm_in", 1, F32)
         warm_out = tile("warm_out", 1, F32)
@@ -72,33 +83,35 @@ def tile_picked_dhhzmthpolarecpx_none_p_kernel(
         xs = load_scale_table("xs", x_scales)
         l_offs = load_list("offs", offs)
         l_hz = load_list("hz", hz)
-        ws_raw = [load_scale_table(name, src) for name, src in (("w1s_raw", w1_scales), ("w2s_raw", w2_scales))]
+        ws_raw = tile("ws_raw", 2 * H, U8)
+        for i, src in enumerate((w1_scales, w2_scales)):
+            load_scale_rows(ws_raw[:, i * H : (i + 1) * H], src)
         l_n1 = load_list("n1", n1)
-        l_n2 = load_list("n2", n2)
         xw = load_words("xw", x_words)
         w1_raw = load_words("w1_raw", w1_words)
         w2_raw = load_words("w2_raw", w2_words)
+        l_n2 = load_list("n2", n2)
         l_two = load_list("two", two)
         l_hy = load_list("hy", hy)
         plane_y = zeroed_plane("plane_y", 2 * S + 2 * H)
         plane_x = zeroed_plane("plane_x", 2 * S)
-        plane_a = zeroed_plane("plane_a", 5 * HALF)
+        plane_a = zeroed_plane("plane_a", 2 * H + HALF)
         plane_b = zeroed_plane("plane_b", HALF)
 
-        picked_offs = tile("picked_offs", S, U8, "hold_ds")
-        picked_hz = tile("picked_hz", S, U8, "hold_dw")
-        gather(picked_offs[:], xs, l_offs[:])
-        gather(picked_hz[:], xs, l_hz[:])
+        picked_y = tile("picked_y", 2 * S, U8)
+        gather(picked_y[:, 0:S], xs, l_offs[:])
+        gather(picked_y[:, S : 2 * S], xs, l_hz[:])
         stage = tile("stage", 2 * S + 2 * H, U8)
-        for i, raw in enumerate(ws_raw):
-            dealt = stage[:, 2 * S + i * H : 2 * S + (i + 1) * H]
-            nc.vector.tensor_copy(dealt.rearrange("p (t m) -> p m t", t=TILES), raw[:].rearrange("p (m t) -> p m t", t=TILES))
-        nc.vector.tensor_copy(stage[:, 0:S], picked_offs[:])
-        nc.vector.tensor_copy(stage[:, S : 2 * S], picked_hz[:])
-        move_rows(plane_y, stage, [nc.sync])
+        nc.vector.tensor_copy(
+            stage[:, 2 * S : 2 * S + 2 * H].rearrange("p (w t m) -> p w m t", w=2, t=TILES),
+            ws_raw[:].rearrange("p (w m t) -> p w m t", w=2, t=TILES),
+        )
+        nc.vector.tensor_copy(stage[:, 0 : 2 * S].bitcast(I32), picked_y[:].bitcast(I32))
+        move_rows(plane_y, stage)
+
         l_k = [load_list(name, src) for name, src in (("k1", k1), ("k2", k2), ("k3", k3))]
-        ds = load_scale_table("ds", d_scales, "hold_ds")
-        dw = load_words("dw", d_words, "hold_dw")
+        ds = load_scale_table("ds", d_scales, after="picked_y")
+        dw = load_words("dw", d_words, after="stage")
 
         x_offs = tile("x_offs", S, U32)
         x_hz = tile("x_hz", S, U32)
@@ -112,11 +125,17 @@ def tile_picked_dhhzmthpolarecpx_none_p_kernel(
         y_ps = []
         for t in range(TILES):
             acc = psum.tile([P, S], F32, name=f"y_ps{t}", tag=f"y_ps{t}")
-            cols = slice(t * P, (t + 1) * P)
-            nc.tensor.matmul_mx(acc[:], lhsT=w1[:, cols].bitcast(FP8X4), lhsT_scale=plane_y[:, 2 * S + t * P : 2 * S + (t + 1) * P],
-                                rhs=x_offs[:].bitcast(FP8X4), rhs_scale=plane_y[:, 0:S], start=True, stop=False)
-            nc.tensor.matmul_mx(acc[:], lhsT=w2[:, cols].bitcast(FP8X4), lhsT_scale=plane_y[:, 2 * S + H + t * P : 2 * S + H + (t + 1) * P],
-                                rhs=x_hz[:].bitcast(FP8X4), rhs_scale=plane_y[:, S : 2 * S], start=False, stop=True)
+            for i, (weights, picked) in enumerate(((w1, x_offs), (w2, x_hz))):
+                scale_col = 2 * S + i * H + t * P
+                nc.tensor.matmul_mx(
+                    acc[:],
+                    lhsT=weights[:, t * P : (t + 1) * P].bitcast(FP8X4),
+                    lhsT_scale=plane_y[:, scale_col : scale_col + P],
+                    rhs=picked[:].bitcast(FP8X4),
+                    rhs_scale=plane_y[:, i * S : (i + 1) * S],
+                    start=(i == 0),
+                    stop=(i == 1),
+                )
             y_ps.append(acc)
 
         l_n3 = load_list("n3", n3)
@@ -124,9 +143,9 @@ def tile_picked_dhhzmthpolarecpx_none_p_kernel(
         l_n5 = load_list("n5", n5)
         l_n6 = load_list("n6", n6)
         l_n7 = load_list("n7", n7)
-        gs_t = tile("gs_t", TILES, F32, "x_offs")
-        sl_t = tile("sl_t", TILES, F32, "x_hz")
-        th_t = tile("th_t", TILES, F32, "w1")
+        gs_t = tile("gs_t", TILES, F32, after="x_offs")
+        sl_t = tile("sl_t", TILES, F32, after="x_hz")
+        th_t = tile("th_t", TILES, F32, after="w1")
         nc.sync.dma_start(gs_t[:], gs.rearrange("(p t) o -> p (t o)", t=TILES))
         with nc.allow_non_contiguous_dma(reason="one value a row, rows 128 t + p"):
             nc.sync.dma_start(sl_t[:], sl.rearrange("(t p) o -> p (t o)", t=TILES))
@@ -137,15 +156,21 @@ def tile_picked_dhhzmthpolarecpx_none_p_kernel(
         picked_x = tile("picked_x", 2 * S, U8)
         gather(picked_x[:, 0:S], xs, l_two[:])
         gather(picked_x[:, S : 2 * S], xs, l_hy[:])
-        move_rows(plane_x, picked_x, [nc.sync])
+        move_rows(plane_x, picked_x)
         gather(x_two[:], xw, l_two[:])
         gather(x_hy[:], xw, l_hy[:])
 
         z = tile("z", TILES * S, BF16)
         z_view = z[:].rearrange("p (j t) -> p j t", t=TILES)
-        pairs, roots, rests, ubs, wide = {}, {}, {}, {}, {}
 
-        def fetch_y(t):
+        picked_k1 = tile("picked_k1", H, U8)
+        gather(picked_k1[:], ds, l_k[K1][:])
+        move_rows(plane_a[:, 0:H], picked_k1)
+
+        y_pairs, squares, ubs, wide = [], [], [], []
+        RB, RA = slice(S, S + W), slice(S + W, 2 * S)
+
+        for t in range(TILES):
             y = tile(f"y{t}", S, F32)
             if t == 0:
                 nc.scalar.copy(y[:], y_ps[t][:])
@@ -154,91 +179,86 @@ def tile_picked_dhhzmthpolarecpx_none_p_kernel(
             pair = tile(f"pair{t}", 2 * W, F32)
             nc.scalar.activation(pair[:, 0:W], y[:].indirect(l_n1[:]), ACT.Copy)
             nc.scalar.activation(pair[:, W : 2 * W], y[:].indirect(l_n2[:]), ACT.Copy)
-            pairs[t] = pair
+            y_pairs.append(pair)
 
-        def polar(t):
-            pair = pairs[t]
+        for t in range(TILES):
+            pair = y_pairs[t]
             sq = tile(f"sq{t}", 2 * W, F32)
             nc.vector.tensor_tensor(sq[:], pair[:], pair[:], ALU.mult)
-            wide[t] = tile(f"wide{t}", 2 * S, F32)
-            rest = wide[t][:, S : S + W]
-            nc.vector.scalar_tensor_tensor(rest, pair[:, 0:W], -0.5, pair[:, W : 2 * W], ALU.mult, ALU.add)
+            wide.append(tile(f"wide{t}", 2 * S, F32))
+            nc.vector.scalar_tensor_tensor(wide[t][:, RB], pair[:, 0:W], -0.5, pair[:, W : 2 * W], ALU.mult, ALU.add)
             ssum = tile(f"ssum{t}", W, F32)
             nc.vector.scalar_tensor_tensor(ssum[:], sq[:, 0:W], 0.25, sq[:, W : 2 * W], ALU.add, ALU.add)
-            roots[t], rests[t] = ssum, rest
+            squares.append(ssum)
 
-        def place_u(t):
-            root = wide[t][:, S + W : 2 * S]
-            nc.scalar.activation(root, roots[t][:], ACT.Sqrt)
+        for t in range(TILES):
+            nc.scalar.activation(wide[t][:, RA], squares[t][:], ACT.Sqrt)
             ub = tile(f"ub{t}", S, F32)
-            nc.scalar.activation(ub[:].indirect(l_n2[:]), rests[t], ACT.Copy)
-            nc.scalar.activation(ub[:].indirect(l_n1[:]), root, ACT.Copy)
-            ubs[t] = ub
+            nc.scalar.activation(ub[:].indirect(l_n2[:]), wide[t][:, RB], ACT.Copy)
+            nc.scalar.activation(ub[:].indirect(l_n1[:]), wide[t][:, RA], ACT.Copy)
+            ubs.append(ub)
+
+        def pick_d(name, matrix, half, after):
+            words = tile(name, HALF, U32, after)
+            gather(words[:], dw, list_half(l_k[matrix], half))
+            return words
+
+        picked_a = tile("picked_a", H + HALF, U8, after="sq1")
+        gather(picked_a[:, 0:H], ds, l_k[K2][:])
+        gather(picked_a[:, H : H + HALF], ds, list_half(l_k[K3], 0))
+        move_rows(plane_a[:, H : 2 * H + HALF], picked_a)
+        d_first = {m: pick_d(f"d_a{m}", m, 0, after) for m, after in ((K2, "sq2"), (K3, "pair2"), (K1, "pair3"))}
 
         def weigh(t, cols):
             nc.vector.tensor_scalar(z_view[:, cols, t], ubs[t][:, cols], gs_t[:, t : t + 1], None, ALU.mult)
 
-        def pick_d(name, i, half, tag):
-            dst = tile(name, HALF, U32, tag)
-            gather(dst[:], dw, l_k[i][:, 16 * half : 16 * half + 16])
-            return dst
-
-        picked_k1 = tile("picked_k1", H, U8)
-        gather(picked_k1[:], ds, l_k[0][:])
-        move_rows(plane_a[:, 0:H], picked_k1, [nc.sync])
-        for step in (fetch_y, polar, place_u):
-            for t in range(TILES):
-                step(t)
-
-        picked_a = tile("picked_a", 3 * HALF, U8, "sq1")
-        gather(picked_a[:, 0:H], ds, l_k[1][:])
-        gather(picked_a[:, H : H + HALF], ds, l_k[2][:, 0:16])
-        move_rows(plane_a[:, H : 5 * HALF], picked_a, [nc.sync])
-        d_a = {i: pick_d(f"d_a{i}", i, 0, tag) for i, tag in ((1, "sq2"), (2, "pair2"), (0, "pair3"))}
-
-        bias = tile("bias", TILES, F32)
-        nc.vector.scalar_tensor_tensor(bias[:], sl_t[:], -1.0, th_t[:], ALU.mult, ALU.mult)
         for t in range(TILES - 1):
             weigh(t, slice(0, S))
-        weigh(TILES - 1, slice(0, W))
-        weigh(TILES - 1, slice(W, S))
+        bias = tile("bias", TILES, F32, after="ub1")
+        nc.vector.scalar_tensor_tensor(bias[:], sl_t[:], -1.0, th_t[:], ALU.mult, ALU.mult)
+
+        halves = (slice(0, W), slice(W, S))
+        for cols in halves:
+            weigh(TILES - 1, cols)
         z_codes = tile("z_codes", S, U32)
         z_plane = tile("z_plane", S, U8)
-        for u in range(2):
-            cols = slice(u * W, (u + 1) * W)
-            nc.vector.quantize_mx(out=z_codes[:, cols].bitcast(FP8X4), scales=z_plane[:, cols], in_=z[:, TILES * u * W : TILES * (u + 1) * W])
+        for cols in halves:
+            nc.vector.quantize_mx(
+                out=z_codes[:, cols].bitcast(FP8X4), scales=z_plane[:, cols], in_=z[:, TILES * cols.start : TILES * cols.stop]
+            )
 
-        picked_b = tile("picked_b", HALF, U8, "z")
-        gather(picked_b[:], ds, l_k[2][:, 16:32])
-        move_rows(plane_b, picked_b, [nc.sync])
+        picked_b = tile("picked_b", HALF, U8, after="z")
+        gather(picked_b[:], ds, list_half(l_k[K3], 1))
+        move_rows(plane_b, picked_b)
 
-        h2s, sts, pairs2, results = {}, {}, {}, {}
+        sts, results = {}, {}
 
         def product(t, d_codes):
             acc = psum.tile([P, S], F32, name=f"h_ps{t}", tag=f"h_ps{t}")
-            moving = (
-                (1, x_two[:], plane_x[:, 0:S], slice(0, S)),
-                (2, x_hy[:], plane_x[:, S : 2 * S], slice(0, S)),
-                (0, z_codes[:, 0:W], z_plane[:, 0:W], slice(0, W)),
-                (0, z_codes[:, W:S], z_plane[:, W:S], slice(W, S)),
-            )
-            for n, (i, codes, plane, cols) in enumerate(moving):
-                c0 = (t % 2) * P
-                if i == 2 and t >= 2:
-                    d_plane = plane_b[:, (t - 2) * P : (t - 1) * P]
+            half, first_col = t // 2, (t % 2) * P
+            passes = [(K2, x_two[:], plane_x[:, 0:S], slice(0, S)), (K3, x_hy[:], plane_x[:, S : 2 * S], slice(0, S))]
+            passes.extend((K1, z_codes[:, cols], z_plane[:, cols], cols) for cols in halves)
+            for n, (matrix, codes, plane, cols) in enumerate(passes):
+                if matrix == K3 and half == 1:
+                    d_plane = plane_b[:, first_col : first_col + P]
                 else:
-                    d_plane = plane_a[:, i * H + t * P : i * H + (t + 1) * P]
-                nc.tensor.matmul_mx(acc[:, cols], lhsT=d_codes[i][:, c0 : c0 + P].bitcast(FP8X4), lhsT_scale=d_plane,
-                                    rhs=codes.bitcast(FP8X4), rhs_scale=plane, start=(n == 0), stop=(n == 3))
-            h2 = wide[t][:, 0:S]
-            nc.vector.tensor_scalar(h2, acc[:], 0.0625, None, ALU.mult)
-            h2s[t] = h2
+                    d_plane = plane_a[:, matrix * H + t * P : matrix * H + (t + 1) * P]
+                nc.tensor.matmul_mx(
+                    acc[:, cols],
+                    lhsT=d_codes[matrix][:, first_col : first_col + P].bitcast(FP8X4),
+                    lhsT_scale=d_plane,
+                    rhs=codes.bitcast(FP8X4),
+                    rhs_scale=plane,
+                    start=(n == 0),
+                    stop=(n == len(passes) - 1),
+                )
+            nc.vector.tensor_scalar(wide[t][:, 0:S], acc[:], 0.0625, None, ALU.mult)
 
         def gate(t):
             sg = tile(f"sg{t}", S, F32)
             nc.scalar.activation(sg[:], wide[t][:].indirect(l_n3[:]), ACT.Sigmoid, bias=bias[:, t : t + 1], scale=sl_t[:, t : t + 1])
             st = tile(f"st{t}", S, F32)
-            nc.vector.tensor_tensor(st[:], h2s[t], sg[:], ALU.mult)
+            nc.vector.tensor_tensor(st[:], wide[t][:, 0:S], sg[:], ALU.mult)
             sts[t] = st
 
         def fetch_st(t):
@@ -249,30 +269,30 @@ def tile_picked_dhhzmthpolarecpx_none_p_kernel(
             diff = tile(f"diff{t}", W, F32)
             nc.vector.tensor_tensor(larger[:], pair[:, 0:W], pair[:, W : 2 * W], ALU.max)
             nc.vector.tensor_tensor(diff[:], pair[:, 0:W], pair[:, W : 2 * W], ALU.subtract)
-            pairs2[t] = (larger, diff)
+            results[t] = (larger, diff)
 
         def place_out(t):
+            larger, diff = results[t]
             res = tile(f"res{t}", S, F32)
-            nc.scalar.activation(res[:].indirect(l_n6[:]), pairs2[t][0][:], ACT.Copy)
-            nc.scalar.activation(res[:].indirect(l_n7[:]), pairs2[t][1][:], ACT.Copy)
+            nc.scalar.activation(res[:].indirect(l_n6[:]), larger[:], ACT.Copy)
+            nc.scalar.activation(res[:].indirect(l_n7[:]), diff[:], ACT.Copy)
             nc.sync.dma_start(out[t * P : (t + 1) * P, :], res[:])
 
-        product(0, d_a)
-        product(1, d_a)
-        d_b = {1: pick_d("d_b1", 1, 1, "pair3")}
+        d_second = {}
+        product(0, d_first)
+        product(1, d_first)
+        d_second[K2] = pick_d("d_b1", K2, 1, after="pair3")
         gate(0)
         gate(1)
         fetch_st(0)
-        d_b[2] = pick_d("d_b2", 2, 1, "pair2_0")
+        d_second[K3] = pick_d("d_b2", K3, 1, after="pair2_0")
         fetch_st(1)
-        d_b[0] = pick_d("d_b0", 0, 1, "pair2_1")
+        d_second[K1] = pick_d("d_b0", K1, 1, after="pair2_1")
         place_out(0)
         place_out(1)
-        product(2, d_b)
-        product(3, d_b)
-        gate(2)
-        gate(3)
-        fetch_st(2)
-        fetch_st(3)
-        place_out(2)
-        place_out(3)
+
+        for t in (2, 3):
+            product(t, d_second)
+        for step in (gate, fetch_st, place_out):
+            for t in (2, 3):
+                step(t)

from contextlib import ExitStack

import concourse.mybir as mybir

K, S, H, W = 512, 256, 512, 128
FLOPS = 5 * 2 * K * H * S

F32 = mybir.dt.float32
BF16 = mybir.dt.bfloat16
I32 = mybir.dt.int32
U32 = mybir.dt.uint32
U16 = mybir.dt.uint16
U8 = mybir.dt.uint8
FP8X4 = mybir.dt.float8_e4m3fn_x4
ALU = mybir.AluOpType
ACT = mybir.ActivationFunctionType

P = 128
TILES = 4
QUADRANTS = 4
BLOCK_PARTITIONS = 8
SCALE_ROWS = 16
HALF = H // 2
HALF_COLS = HALF // 16
K1, K2, K3 = 0, 1, 2


def tile_picked_dhhzmthpolarecpx_none_p_kernel(
    tc, x_words, x_scales, w1_words, w1_scales, w2_words, w2_scales, gs, d_words, d_scales, sl, th,
    offs, hz, n1, n2, k1, k2, two, k3, hy, n3, n4, n5, n6, n7, out,
):
    nc = tc.nc
    with ExitStack() as ctx:
        lists = ctx.enter_context(tc.tile_pool(name="lists", bufs=1))
        sb = ctx.enter_context(tc.tile_pool(name="sb", bufs=1))
        psum = ctx.enter_context(tc.psum_pool(name="psum", bufs=1))

        def tile(name, cols, dtype, after=None):
            return sb.tile([P, cols], dtype, name=name, tag=after or name, align_bytes=64)

        def load_list(name, src):
            offsets = lists.tile(list(src.shape), U16, name="list_" + name, tag="list_" + name)
            nc.sync.dma_start(offsets[:], src)
            return offsets

        def load_words(name, src, after=None):
            words = tile(name, src.shape[2], U32, after)
            nc.sync.dma_start(words[:].bitcast(I32), src[0].rearrange("p n t -> p (n t)").bitcast(I32))
            return words

        def load_scale_rows(dst, src):
            rows = src[0].bitcast(I32)
            nc.sync.dma_start(dst.bitcast(I32), rows.unsqueeze(1).to_broadcast([SCALE_ROWS, BLOCK_PARTITIONS, src.shape[2] // 4]))

        def load_scale_table(name, src, after=None):
            table = tile(name, src.shape[2], U8, after)
            load_scale_rows(table[:], src)
            return table

        def zeroed_plane(name, cols):
            plane = tile(name, cols, U8)
            nc.vector.memset(plane[:].bitcast(I32), 0)
            return plane

        def move_rows(plane, table_layout):
            for q in range(QUADRANTS):
                nc.sync.dma_start(
                    plane[32 * q : 32 * q + 4, :].bitcast(I32),
                    table_layout[32 * q : 32 * q + 32 : BLOCK_PARTITIONS, :].bitcast(I32),
                )

        def gather(dst, table, offsets):
            nc.vector.tensor_copy(dst, table[:].indirect(offsets))

        def list_half(offsets, half):
            return offsets[:, half * HALF_COLS : (half + 1) * HALF_COLS]

        warm_in = tile("warm_in", 1, F32)
        warm_out = tile("warm_out", 1, F32)
        nc.vector.memset(warm_in[:], 1.0)
        nc.scalar.activation(warm_out[:], warm_in[:], ACT.Sqrt)

        xs = load_scale_table("xs", x_scales)
        l_offs = load_list("offs", offs)
        l_hz = load_list("hz", hz)
        ws_raw = tile("ws_raw", 2 * H, U8)
        for i, src in enumerate((w1_scales, w2_scales)):
            load_scale_rows(ws_raw[:, i * H : (i + 1) * H], src)
        l_n1 = load_list("n1", n1)
        xw = load_words("xw", x_words)
        w1_raw = load_words("w1_raw", w1_words)
        w2_raw = load_words("w2_raw", w2_words)
        l_n2 = load_list("n2", n2)
        l_two = load_list("two", two)
        l_hy = load_list("hy", hy)
        plane_y = zeroed_plane("plane_y", 2 * S + 2 * H)
        plane_x = zeroed_plane("plane_x", 2 * S)
        plane_a = zeroed_plane("plane_a", 2 * H + HALF)
        plane_b = zeroed_plane("plane_b", HALF)

        picked_y = tile("picked_y", 2 * S, U8)
        gather(picked_y[:, 0:S], xs, l_offs[:])
        gather(picked_y[:, S : 2 * S], xs, l_hz[:])
        stage = tile("stage", 2 * S + 2 * H, U8)
        nc.vector.tensor_copy(
            stage[:, 2 * S : 2 * S + 2 * H].rearrange("p (w t m) -> p w m t", w=2, t=TILES),
            ws_raw[:].rearrange("p (w m t) -> p w m t", w=2, t=TILES),
        )
        nc.vector.tensor_copy(stage[:, 0 : 2 * S].bitcast(I32), picked_y[:].bitcast(I32))
        move_rows(plane_y, stage)

        l_k = [load_list(name, src) for name, src in (("k1", k1), ("k2", k2), ("k3", k3))]
        ds = load_scale_table("ds", d_scales, after="picked_y")
        dw = load_words("dw", d_words, after="stage")

        x_offs = tile("x_offs", S, U32)
        x_hz = tile("x_hz", S, U32)
        gather(x_offs[:], xw, l_offs[:])
        gather(x_hz[:], xw, l_hz[:])
        w1 = tile("w1", H, U32)
        w2 = tile("w2", H, U32)
        for dealt, raw in ((w1, w1_raw), (w2, w2_raw)):
            nc.scalar.copy(dealt[:].rearrange("p (t m) -> p m t", t=TILES), raw[:].rearrange("p (m t) -> p m t", t=TILES))

        y_ps = []
        for t in range(TILES):
            acc = psum.tile([P, S], F32, name=f"y_ps{t}", tag=f"y_ps{t}")
            for i, (weights, picked) in enumerate(((w1, x_offs), (w2, x_hz))):
                scale_col = 2 * S + i * H + t * P
                nc.tensor.matmul_mx(
                    acc[:],
                    lhsT=weights[:, t * P : (t + 1) * P].bitcast(FP8X4),
                    lhsT_scale=plane_y[:, scale_col : scale_col + P],
                    rhs=picked[:].bitcast(FP8X4),
                    rhs_scale=plane_y[:, i * S : (i + 1) * S],
                    start=(i == 0),
                    stop=(i == 1),
                )
            y_ps.append(acc)

        l_n3 = load_list("n3", n3)
        l_n4 = load_list("n4", n4)
        l_n5 = load_list("n5", n5)
        l_n6 = load_list("n6", n6)
        l_n7 = load_list("n7", n7)
        gs_t = tile("gs_t", TILES, F32, after="x_offs")
        sl_t = tile("sl_t", TILES, F32, after="x_hz")
        th_t = tile("th_t", TILES, F32, after="w1")
        nc.sync.dma_start(gs_t[:], gs.rearrange("(p t) o -> p (t o)", t=TILES))
        with nc.allow_non_contiguous_dma(reason="one value a row, rows 128 t + p"):
            nc.sync.dma_start(sl_t[:], sl.rearrange("(t p) o -> p (t o)", t=TILES))
            nc.sync.dma_start(th_t[:], th.rearrange("(t p) o -> p (t o)", t=TILES))

        x_two = tile("x_two", S, U32)
        x_hy = tile("x_hy", S, U32)
        picked_x = tile("picked_x", 2 * S, U8)
        gather(picked_x[:, 0:S], xs, l_two[:])
        gather(picked_x[:, S : 2 * S], xs, l_hy[:])
        move_rows(plane_x, picked_x)
        gather(x_two[:], xw, l_two[:])
        gather(x_hy[:], xw, l_hy[:])

        z = tile("z", TILES * S, BF16)
        z_view = z[:].rearrange("p (j t) -> p j t", t=TILES)

        picked_k1 = tile("picked_k1", H, U8)
        gather(picked_k1[:], ds, l_k[K1][:])
        move_rows(plane_a[:, 0:H], picked_k1)

        y_pairs, squares, ubs, wide = [], [], [], []
        RB, RA = slice(S, S + W), slice(S + W, 2 * S)

        for t in range(TILES):
            y = tile(f"y{t}", S, F32)
            if t == 0:
                nc.scalar.copy(y[:], y_ps[t][:])
            else:
                nc.vector.tensor_copy(y[:], y_ps[t][:])
            pair = tile(f"pair{t}", 2 * W, F32)
            nc.scalar.activation(pair[:, 0:W], y[:].indirect(l_n1[:]), ACT.Copy)
            nc.scalar.activation(pair[:, W : 2 * W], y[:].indirect(l_n2[:]), ACT.Copy)
            y_pairs.append(pair)

        for t in range(TILES):
            pair = y_pairs[t]
            sq = tile(f"sq{t}", 2 * W, F32)
            nc.vector.tensor_tensor(sq[:], pair[:], pair[:], ALU.mult)
            wide.append(tile(f"wide{t}", 2 * S, F32))
            nc.vector.scalar_tensor_tensor(wide[t][:, RB], pair[:, 0:W], -0.5, pair[:, W : 2 * W], ALU.mult, ALU.add)
            ssum = tile(f"ssum{t}", W, F32)
            nc.vector.scalar_tensor_tensor(ssum[:], sq[:, 0:W], 0.25, sq[:, W : 2 * W], ALU.add, ALU.add)
            squares.append(ssum)

        for t in range(TILES):
            nc.scalar.activation(wide[t][:, RA], squares[t][:], ACT.Sqrt)
            ub = tile(f"ub{t}", S, F32)
            nc.scalar.activation(ub[:].indirect(l_n2[:]), wide[t][:, RB], ACT.Copy)
            nc.scalar.activation(ub[:].indirect(l_n1[:]), wide[t][:, RA], ACT.Copy)
            ubs.append(ub)

        def pick_d(name, matrix, half, after):
            words = tile(name, HALF, U32, after)
            gather(words[:], dw, list_half(l_k[matrix], half))
            return words

        picked_a = tile("picked_a", H + HALF, U8, after="sq1")
        gather(picked_a[:, 0:H], ds, l_k[K2][:])
        gather(picked_a[:, H : H + HALF], ds, list_half(l_k[K3], 0))
        move_rows(plane_a[:, H : 2 * H + HALF], picked_a)
        d_first = {m: pick_d(f"d_a{m}", m, 0, after) for m, after in ((K2, "sq2"), (K3, "pair2"), (K1, "pair3"))}

        def weigh(t, cols):
            nc.vector.tensor_scalar(z_view[:, cols, t], ubs[t][:, cols], gs_t[:, t : t + 1], None, ALU.mult)

        for t in range(TILES - 1):
            weigh(t, slice(0, S))
        bias = tile("bias", TILES, F32, after="ub1")
        nc.vector.scalar_tensor_tensor(bias[:], sl_t[:], -1.0, th_t[:], ALU.mult, ALU.mult)

        halves = (slice(0, W), slice(W, S))
        for cols in halves:
            weigh(TILES - 1, cols)
        z_codes = tile("z_codes", S, U32)
        z_plane = tile("z_plane", S, U8)
        for cols in halves:
            nc.vector.quantize_mx(
                out=z_codes[:, cols].bitcast(FP8X4), scales=z_plane[:, cols], in_=z[:, TILES * cols.start : TILES * cols.stop]
            )

        picked_b = tile("picked_b", HALF, U8, after="z")
        gather(picked_b[:], ds, list_half(l_k[K3], 1))
        move_rows(plane_b, picked_b)

        sts, results = {}, {}

        def product(t, d_codes):
            acc = psum.tile([P, S], F32, name=f"h_ps{t}", tag=f"h_ps{t}")
            half, first_col = t // 2, (t % 2) * P
            passes = [(K2, x_two[:], plane_x[:, 0:S], slice(0, S)), (K3, x_hy[:], plane_x[:, S : 2 * S], slice(0, S))]
            passes.extend((K1, z_codes[:, cols], z_plane[:, cols], cols) for cols in halves)
            for n, (matrix, codes, plane, cols) in enumerate(passes):
                if matrix == K3 and half == 1:
                    d_plane = plane_b[:, first_col : first_col + P]
                else:
                    d_plane = plane_a[:, matrix * H + t * P : matrix * H + (t + 1) * P]
                nc.tensor.matmul_mx(
                    acc[:, cols],
                    lhsT=d_codes[matrix][:, first_col : first_col + P].bitcast(FP8X4),
                    lhsT_scale=d_plane,
                    rhs=codes.bitcast(FP8X4),
                    rhs_scale=plane,
                    start=(n == 0),
                    stop=(n == len(passes) - 1),
                )
            nc.vector.tensor_scalar(wide[t][:, 0:S], acc[:], 0.0625, None, ALU.mult)

        def gate(t):
            sg = tile(f"sg{t}", S, F32)
            nc.scalar.activation(sg[:], wide[t][:].indirect(l_n3[:]), ACT.Sigmoid, bias=bias[:, t : t + 1], scale=sl_t[:, t : t + 1])
            st = tile(f"st{t}", S, F32)
            nc.vector.tensor_tensor(st[:], wide[t][:, 0:S], sg[:], ALU.mult)
            sts[t] = st

        def fetch_st(t):
            pair = tile(f"pair2_{t}", 2 * W, F32)
            nc.scalar.activation(pair[:, 0:W], sts[t][:].indirect(l_n4[:]), ACT.Copy)
            nc.scalar.activation(pair[:, W : 2 * W], sts[t][:].indirect(l_n5[:]), ACT.Copy)
            larger = tile(f"larger{t}", W, F32)
            diff = tile(f"diff{t}", W, F32)
            nc.vector.tensor_tensor(larger[:], pair[:, 0:W], pair[:, W : 2 * W], ALU.max)
            nc.vector.tensor_tensor(diff[:], pair[:, 0:W], pair[:, W : 2 * W], ALU.subtract)
            results[t] = (larger, diff)

        def place_out(t):
            larger, diff = results[t]
            res = tile(f"res{t}", S, F32)
            nc.scalar.activation(res[:].indirect(l_n6[:]), larger[:], ACT.Copy)
            nc.scalar.activation(res[:].indirect(l_n7[:]), diff[:], ACT.Copy)
            nc.sync.dma_start(out[t * P : (t + 1) * P, :], res[:])

        d_second = {}
        product(0, d_first)
        product(1, d_first)
        d_second[K2] = pick_d("d_b1", K2, 1, after="pair3")
        gate(0)
        gate(1)
        fetch_st(0)
        d_second[K3] = pick_d("d_b2", K3, 1, after="pair2_0")
        fetch_st(1)
        d_second[K1] = pick_d("d_b0", K1, 1, after="pair2_1")
        place_out(0)
        place_out(1)

        for t in (2, 3):
            product(t, d_second)
        for step in (gate, fetch_st, place_out):
            for t in (2, 3):
                step(t)
